import numpy as np
import ml_dtypes


def mxq(x, axis, fmt="e4m3"):
    dtype, down = {"e4m3": (ml_dtypes.float8_e4m3fn, 7), "e5m2": (ml_dtypes.float8_e5m2, 14)}[fmt]
    v = np.moveaxis(np.asarray(x, np.float32).astype(ml_dtypes.bfloat16).astype(np.float64), axis, -1)
    blocks = v.reshape(v.shape[:-1] + (-1, 32))
    amax = np.abs(blocks).max(-1, keepdims=True)
    byte = np.maximum(np.where(amax > 0, np.frexp(amax)[1] - 1 + 127, 0) - down, 1)
    scale = np.exp2(byte - 127.0)
    codes = (blocks / scale).astype(np.float32).astype(dtype).astype(np.float64)
    return np.moveaxis((codes * scale).reshape(v.shape), -1, axis)


WIDE = False


def mx_kscale(k):
    if not WIDE:
        return np.ones(k)
    levels = np.array([10, -10, 5, -5, 0])
    if k % 512:
        return np.exp2(np.random.permutation(np.resize(levels, k // 32))).repeat(32)
    a = np.empty((k // 512, 16))
    for p in range(k // 512):
        a[p, :8] = np.random.permutation(np.resize(levels, 8))
        for g in range(8):
            far = levels[np.abs(levels - a[p, g]) >= 10]
            a[p, g + 8] = far[np.random.randint(len(far))]
    return np.exp2(a.ravel()).repeat(32)


def f64(x):
    return np.asarray(x).astype(np.float64)


def striped(idx):
    return np.tile(idx.reshape(-1, 16).T, (8, 1)).astype(np.uint16)


def unstriped(offs):
    return offs[:16].T.reshape(-1).astype(np.int64)


def striped8(idx):
    return np.concatenate([x.reshape(-1, 16).T for x in idx]).astype(np.uint16)


def runs(offs, k):
    lists = np.stack([offs[16 * r : 16 * r + 16].T.reshape(-1) for r in range(8)]).astype(np.int64)
    return lists[np.arange(k) % 512 // 64]


def pack_weight(w):
    k, n = w.shape
    w = f64(np.asarray(w, np.float32).astype(ml_dtypes.bfloat16)).reshape(k // 32, 32, n)
    amax = np.abs(w).max(1)
    byte = np.clip(np.where(amax > 0, np.frexp(amax)[1] - 1 + 127 - 7, 1), 1, 254)
    scaled = (w * np.exp2(127.0 - byte)[:, None, :]).reshape(k, n).astype(np.float32)
    words = np.ascontiguousarray(scaled.reshape(k // 512, 128, 4, n).transpose(0, 1, 3, 2)).astype(ml_dtypes.float8_e4m3fn).view(np.uint8)
    return words, np.ascontiguousarray(byte.astype(np.uint8).reshape(k // 512, 16, n))


def unpack_weight(words, scales):
    g, p, n, _ = words.shape
    vals = np.ascontiguousarray(words).view(ml_dtypes.float8_e4m3fn).astype(np.float64) * np.repeat(np.exp2(scales.astype(np.float64) - 127.0), 8, axis=1)[..., None]
    return vals.transpose(0, 1, 3, 2).reshape(g * 512, n)


E2M1 = np.array([0.0, 0.5, 1.0, 1.5, 2.0, 3.0, 4.0, 6.0, -0.0, -0.5, -1.0, -1.5, -2.0, -3.0, -4.0, -6.0])


def pack_fp4(w):
    k, n = w.shape
    w = f64(np.asarray(w, np.float32).astype(ml_dtypes.bfloat16)).reshape(k // 32, 32, n)
    amax = np.abs(w).max(1)
    mant, ex = np.frexp(amax / 6.0)
    byte = np.clip(np.where(amax > 0, np.where(mant > 0.5, ex, ex - 1) + 127, 1), 1, 254)
    scaled = (w * np.exp2(127.0 - byte)[:, None, :]).reshape(k, n).astype(np.float32)
    c = np.ascontiguousarray(scaled.reshape(k // 512, 128, 4, n).transpose(0, 1, 3, 2)).astype(ml_dtypes.float4_e2m1fn).view(np.uint8) & 0xF
    words = (c[..., 0::2] | (c[..., 1::2] << 4)).reshape(k // 512, 128, 2 * n)
    return np.ascontiguousarray(words), np.ascontiguousarray(byte.astype(np.uint8).reshape(k // 512, 16, n))


def unpack_fp4(words, scales):
    g, _, n = scales.shape
    words = np.ascontiguousarray(words).reshape(g, 128, n, 2)
    nib = np.empty((g, 128, n, 4), np.uint8)
    nib[..., 0::2] = words & 0xF
    nib[..., 1::2] = words >> 4
    vals = E2M1[nib] * np.repeat(np.exp2(scales.astype(np.float64) - 127.0), 8, axis=1)[..., None]
    return vals.transpose(0, 1, 3, 2).reshape(g * 512, n)


def sigmoid(v):
    return 1.0 / (1.0 + np.exp(-np.maximum(v, -700.0)))

def planes(y):
    n, m = y.shape
    v = y.astype(np.float32).astype(ml_dtypes.bfloat16).astype(np.float64).reshape(n // 32, 32, m)
    top = np.abs(v).max(1)
    byte = np.clip(np.where(top > 0, np.frexp(top)[1] - 1 + 127 - 7, 1), 1, 254)
    codes = (v * np.exp2(127.0 - byte)[:, None, :]).reshape(n, m).astype(np.float32).astype(ml_dtypes.float8_e4m3fn).view(np.uint8)
    words = codes.reshape(n // 512, 128, 4, m).transpose(0, 1, 3, 2)
    return np.ascontiguousarray(words), np.ascontiguousarray(byte.astype(np.uint8).reshape(n // 512, 16, m))


K, T, S, N, H, J, C, U = 512, 2048, 512, 512, 512, 512, 512, 1024


def setup_inputs():
    n = np.random.standard_normal
    s = mx_kscale(K)[:, None]
    u = mx_kscale(S)
    packed_xT = pack_weight(n((K, T)) * s)
    packed_w1 = pack_fp4(n((K, H)) / np.sqrt(K) / s)
    packed_w2 = pack_fp4(n((C, N)) / np.sqrt(C) / u[:, None])
    return {
        "x_words": packed_xT[0],
        "x_scales": packed_xT[1],
        "w1_words": packed_w1[0],
        "w1_scales": packed_w1[1],
        "tab": np.random.uniform(0.4, 1.4, (H, J)).astype(np.float32),
        "gs": (np.random.uniform(0.5, 1.5, (K, 1)) / s).astype(np.float32),
        "mem": n((C, U)).astype(np.float32),
        "res": (1.5 * n((N, U))).astype(np.float32),
        "gt": (np.random.uniform(0.5, 1.5, (C, 1)) * u[:, None]).astype(np.float32),
        "w2_words": packed_w2[0],
        "w2_scales": packed_w2[1],
        "offs": striped(np.random.permutation(T)[:S]),
        "n1": striped8(np.random.randint(0, J, (8, S))),
        "n2": striped8(np.stack([np.random.permutation(S) for _ in range(8)])),
        "cand": striped(np.random.permutation(T)[:C]),
        "n3": striped8(np.stack([np.random.permutation(U)[:S] for _ in range(8)])),
    }


def reference(x_words, x_scales, w1_words, w1_scales, tab, gs, mem, res, gt, w2_words, w2_scales, offs, n1, n2, cand, n3):
    old = f64(mem)[np.arange(C)[:, None], runs(n3, C)]
    x_cand = unpack_weight(x_words, x_scales)[:, unstriped(cand)]
    xq = unpack_weight(x_words, x_scales)[:, unstriped(offs)]
    y = unpack_fp4(w1_words, w1_scales).T @ xq
    z = f64(gs) * (y * (f64(tab)[np.arange(H)[:, None], runs(n1, H)]) - (0.5 * (y[np.arange(H)[:, None], runs(n2, H)])))
    s = 0.0625 * ((x_cand.T @ mxq(z, 0, "e4m3")))
    nw = old + sigmoid(s) * (s - old)
    pg = f64(mem).copy()
    pg[np.arange(C)[:, None], runs(n3, C)] = nw
    z2 = f64(gt) * pg
    out_0 = f64(res) + (unpack_fp4(w2_words, w2_scales).T @ mxq(z2, 0, "e4m3"))
    return (out_0,) + planes(out_0)

@@ -1,0 +1,280 @@
+from contextlib import ExitStack
+
+import concourse.mybir as mybir
+
+K, T, S, N, H, J, C, U = 512, 2048, 512, 512, 512, 512, 512, 1024
+FLOPS = 2 * (K * H * S + K * C * S + C * N * U)
+
+F32 = mybir.dt.float32
+BF16 = mybir.dt.bfloat16
+I32 = mybir.dt.int32
+U32 = mybir.dt.uint32
+U16 = mybir.dt.uint16
+U8 = mybir.dt.uint8
+FP8X4 = mybir.dt.float8_e4m3fn_x4
+FP4X4 = mybir.dt.float4_e2m1fn_x4
+ALU = mybir.AluOpType
+ACT = mybir.ActivationFunctionType
+
+P = 128
+R = 4
+HALF = S // 2
+CHUNKS = (128, 256, 256, 256, 128)
+
+
+def tile_picked_readkindgpaget_none_po_kernel(
+    tc, x_words, x_scales, w1_words, w1_scales, tab, gs, mem, res, gt, w2_words, w2_scales, offs, n1, n2, cand, n3, out_0, out_1, out_2
+):
+    nc = tc.nc
+    with ExitStack() as ctx:
+        keep = ctx.enter_context(tc.tile_pool(name="keep", bufs=1))
+        psum = ctx.enter_context(tc.psum_pool(name="psum", bufs=1))
+
+        def sb(name, shape, dtype, tag=""):
+            return keep.tile(shape, dtype, name=name, tag=tag or name, align_bytes=64)
+
+        def bank(b, name, shape):
+            return psum.tile(shape, F32, name=name, tag="bank%d" % b)
+
+        def load_list(name, src):
+            tile = sb(name, [P, S // 16], U16)
+            nc.sync.dma_start(tile[:], src)
+            return tile
+
+        def load_scale_rows(queues, tile, src):
+            for q, queue in enumerate(queues):
+                queue.dma_start(tile[32 * q : 32 * q + 4, :].bitcast(I32), src[0, 4 * q : 4 * q + 4, :].bitcast(I32))
+
+        def dealt_rows(src):
+            return src.rearrange("(p t) w -> p t w", t=R)
+
+        xs = sb("xs", [P, T], U8)
+        w1s_raw = sb("w1s_raw", [P, H], U8)
+        w2s_raw = sb("w2s_raw", [P, N], U8)
+        for tile in (xs, w1s_raw, w2s_raw):
+            nc.vector.memset(tile[:].bitcast(I32), 0)
+
+        w1w_raw = sb("w1w_raw", [P, 2 * H], U8)
+        w2w_raw = sb("w2w_raw", [P, 2 * N], U8)
+        xw = sb("xw", [P, T], U32)
+        nc.sync.dma_start(w1w_raw[:].bitcast(I32), w1_words[0].bitcast(I32))
+        nc.sync.dma_start(w2w_raw[:].bitcast(I32), w2_words[0].bitcast(I32))
+        nc.sync.dma_start(xw[:].bitcast(I32), x_words[0].rearrange("p n t -> p (n t)").bitcast(I32))
+        offs_sb = load_list("offs_sb", offs)
+        load_scale_rows([nc.sync] * 4, xs, x_scales)
+        load_scale_rows([nc.sync, nc.sync, nc.gpsimd, nc.gpsimd], w1s_raw, w1_scales)
+        cand_sb = load_list("cand_sb", cand)
+        gs_sb = sb("gs_sb", [P, R], F32)
+        gt_sb = sb("gt_sb", [P, R], F32)
+        nc.sync.dma_start(gs_sb[:], gs.rearrange("(p t) o -> p (t o)", t=R))
+        n1_sb = load_list("n1_sb", n1)
+        n2_sb = load_list("n2_sb", n2)
+
+        tab_raw = [sb("tab_raw%d" % t, [P, J], F32) for t in range(R)]
+        for t in range(R):
+            nc.sync.dma_start(tab_raw[t][:], dealt_rows(tab)[:, t, :])
+        n3_sb = load_list("n3_sb", n3)
+        page = [sb("page%d" % t, [P, U], F32) for t in range(R)]
+        for t in range(R):
+            nc.sync.dma_start(page[t][:], dealt_rows(mem)[:, t, :])
+        load_scale_rows([nc.sync] * 4, w2s_raw, w2_scales)
+        nc.sync.dma_start(gt_sb[:], gt.rearrange("(p t) o -> p (t o)", t=R))
+        starts = [sum(CHUNKS[:c]) for c in range(len(CHUNKS))]
+        cols = [slice(a, a + n) for a, n in zip(starts, CHUNKS)]
+        res_sb = [sb("res%d" % c, [P, R, n], F32) for c, n in enumerate(CHUNKS)]
+        for c in range(len(CHUNKS)):
+            nc.sync.dma_start(res_sb[c][:], dealt_rows(res)[:, :, cols[c]])
+
+        def deal_fp4_words(name, raw):
+            dealt = sb(name, [P, 2 * R * P], U8)
+            nc.vector.tensor_copy(
+                dealt[:].rearrange("p (t m b) -> p m t b", t=R, b=2), raw[:].rearrange("p (m t b) -> p m t b", t=R, b=2)
+            )
+            return dealt
+
+        def deal_bytes(name, raw, tag=""):
+            dealt = sb(name, [P, R * P], U8, tag)
+            nc.vector.tensor_copy(dealt[:].rearrange("p (t m) -> p m t", t=R), raw[:].rearrange("p (m t) -> p m t", t=R))
+            return dealt
+
+        w1w = deal_fp4_words("w1w", w1w_raw)
+        w2w = deal_fp4_words("w2w", w2w_raw)
+
+        xq_w = sb("xq_w", [P, S], U32)
+        xq_s = sb("xq_s", [P, S], U8)
+        nc.vector.tensor_copy(xq_w[:], xw[:].indirect(offs_sb[:]))
+        nc.vector.tensor_copy(xq_s[:], xs[:].indirect(offs_sb[:]))
+        w1s = deal_bytes("w1s", w1s_raw)
+
+        gs_half = sb("gs_half", [P, R], F32)
+        nc.scalar.mul(gs_half[:], gs_sb[:], -0.5)
+        tab2 = [sb("tab2_%d" % t, [P, J], F32) for t in range(R)]
+        for t in range(R):
+            nc.scalar.mul(tab2[t][:], tab_raw[t][:], -2.0)
+
+        y = [sb("y%d" % t, [P, S], F32) for t in range(R)]
+        for t in range(R):
+            acc = bank(t, "y_acc%d" % t, [P, S])
+            nc.tensor.matmul_mx(
+                out=acc[:],
+                lhsT=w1w[:, 2 * P * t : 2 * P * (t + 1)].bitcast(FP4X4),
+                lhsT_scale=w1s[:, P * t : P * (t + 1)],
+                rhs=xq_w[:].bitcast(FP8X4),
+                rhs_scale=xq_s[:],
+                start=True,
+                stop=True,
+            )
+            nc.scalar.activation(y[t][:], acc[:], ACT.Copy, scale=gs_half[:, t : t + 1])
+
+        xc_w = sb("xc_w", [P, C], U32)
+        xc_s_raw = sb("xc_s_raw", [P, C], U8)
+        nc.vector.tensor_copy(xc_w[:].rearrange("p (t m) -> p m t", t=R), xw[:].indirect(cand_sb[:]))
+        nc.vector.tensor_copy(xc_s_raw[:], xs[:].indirect(cand_sb[:]))
+        xc_s = deal_bytes("xc_s", xc_s_raw)
+
+        z = [sb("z%d" % h, [P, R, HALF], F32) for h in range(2)]
+        z_bf = [sb("z_bf%d" % h, [P, HALF, R], BF16) for h in range(2)]
+        zw = sb("zw", [P, S], U32)
+        zs = sb("zs", [P, S], U8)
+        zt = {}
+        keepw = [sb("keepw%d" % t, [P, S], F32) for t in range(R)]
+        fresh = [sb("fresh%d" % t, [P, S], F32) for t in range(R)]
+        first, second, whole = slice(0, HALF), slice(HALF, S), slice(0, S)
+        halves = (first, second)
+
+        def entries(lst, part):
+            return lst[:, part.start // 16 : part.stop // 16]
+
+        def z_first(h, t, tag=""):
+            zt[h, t] = sb("zt%d_%d" % (h, t), [P, HALF], F32, tag)
+            nc.vector.tensor_tensor(zt[h, t][:], tab2[t][:].indirect(entries(n1_sb, halves[h])), y[t][:, halves[h]], ALU.mult)
+
+        def z_second(h, t):
+            nc.vector.tensor_tensor(z[h][:, t, :], y[t][:].indirect(entries(n2_sb, halves[h])), zt[h, t][:], ALU.add)
+
+        def z_round(h):
+            nc.scalar.copy(z_bf[h][:], z[h][:].rearrange("p t j -> p j t"))
+
+        def z_quantize(h):
+            nc.vector.quantize_mx(out=zw[:, halves[h]].bitcast(FP8X4), scales=zs[:, halves[h]], in_=z_bf[h][:].rearrange("p j t -> p (j t)"))
+
+        def scores(t, part, b):
+            n = part.stop - part.start
+            acc = bank(b, "s_acc%d_%d" % (t, part.start), [P, n])
+            nc.tensor.matmul_mx(
+                out=acc[:],
+                lhsT=xc_w[:, P * t : P * (t + 1)].bitcast(FP8X4),
+                lhsT_scale=xc_s[:, P * t : P * (t + 1)],
+                rhs=zw[:, part].bitcast(FP8X4),
+                rhs_scale=zs[:, part],
+                start=True,
+                stop=True,
+            )
+            th = sb("th%d_%d" % (t, part.start), [P, n], F32)
+            nc.scalar.activation(fresh[t][:, part], acc[:], ACT.Silu, scale=0.0625)
+            nc.scalar.activation(th[:], acc[:], ACT.Tanh, scale=0.03125)
+            nc.scalar.activation(keepw[t][:, part], th[:], ACT.Copy, scale=-0.5, bias=0.5)
+
+        for t in range(R + 1):
+            if t < R:
+                z_first(0, t)
+            if t > 0:
+                z_second(0, t - 1)
+        z_round(0)
+        for t in range(R - 1):
+            z_first(1, t)
+        z_quantize(0)
+        scores(0, first, 4)
+        scores(1, first, 5)
+        z_first(1, R - 1, tag="z_bf0")
+        for t in range(R):
+            z_second(1, t)
+        z_round(1)
+
+        kept = {}
+        z2_bf = [sb("z2_bf%d" % c, [P, n, R], BF16) for c, n in enumerate(CHUNKS)]
+
+        def fetch(t, part, tag=""):
+            kept[t, part.start] = sb("kept%d_%d" % (t, part.start), [P, part.stop - part.start], F32, tag)
+            nc.vector.tensor_tensor(kept[t, part.start][:], page[t][:].indirect(entries(n3_sb, part)), keepw[t][:, part], ALU.mult)
+
+        def put(t, part):
+            nc.vector.tensor_tensor(page[t][:].indirect(entries(n3_sb, part)), kept[t, part.start][:], fresh[t][:, part], ALU.add)
+
+        def z2_round(c, t):
+            nc.scalar.activation(z2_bf[c][:, :, t], page[t][:, cols[c]], ACT.Copy, scale=gt_sb[:, t : t + 1])
+
+        fetch(0, first)
+        put(0, first)
+        z_quantize(1)
+        scores(0, second, 6)
+        scores(1, second, 7)
+        scores(2, whole, 0)
+        scores(3, whole, 1)
+        fetch(1, first, tag="z_bf1")
+        put(1, first)
+        for pair, part in (((0, 1), second), ((2, 3), whole)):
+            for t in pair:
+                fetch(t, part)
+            for t in pair:
+                put(t, part)
+                if t < R - 1:
+                    for c in range(len(CHUNKS)):
+                        z2_round(c, t)
+        w2s = deal_bytes("w2s", w2s_raw, tag="kept3_0")
+
+        out_rows = dealt_rows(out_0)
+        out_words = out_1[0].rearrange("p n t -> p (n t)").bitcast(I32)
+        o_scales = sb("o_scales", [P, U], U8)
+        o32 = [sb("o32_%d" % c, [P, R, n], F32) for c, n in enumerate(CHUNKS)]
+        o_bf = [sb("o_bf%d" % c, [P, n, R], BF16) for c, n in enumerate(CHUNKS)]
+        accs = {}
+        last = len(CHUNKS) - 1
+
+        def product(c):
+            n = CHUNKS[c]
+            per_bank = 512 // n
+            z2_round(c, R - 1)
+            z2w = sb("z2w%d" % c, [P, n], U32)
+            z2s = sb("z2s%d" % c, [P, n], U8)
+            nc.vector.quantize_mx(out=z2w[:].bitcast(FP8X4), scales=z2s[:], in_=z2_bf[c][:].rearrange("p j t -> p (j t)"))
+            for t in range(R):
+                if t % per_bank == 0:
+                    acc = bank((2 + len(accs)) % 8, "o_acc%d_%d" % (c, t), [P, per_bank, n])
+                    accs[c, t] = acc
+                nc.tensor.matmul_mx(
+                    out=acc[:, t % per_bank, :],
+                    lhsT=w2w[:, 2 * P * t : 2 * P * (t + 1)].bitcast(FP4X4),
+                    lhsT_scale=w2s[:, P * t : P * (t + 1)],
+                    rhs=z2w[:].bitcast(FP8X4),
+                    rhs_scale=z2s[:],
+                    start=True,
+                    stop=True,
+                )
+
+        def add_res(c):
+            per_bank = 512 // CHUNKS[c]
+            for t in range(0, R, per_bank):
+                rows = slice(t, t + per_bank)
+                nc.vector.tensor_tensor(o32[c][:, rows, :], accs[c, t][:], res_sb[c][:, rows, :], ALU.add)
+            nc.sync.dma_start(out_rows[:, :, cols[c]], o32[c][:])
+            if c < last:
+                nc.scalar.copy(o_bf[c][:], o32[c][:].rearrange("p t w -> p w t"))
+            else:
+                nc.vector.tensor_copy(o_bf[c][:], o32[c][:].rearrange("p t w -> p w t"))
+
+        def planes(c):
+            ow = sb("ow%d" % c, [P, CHUNKS[c]], U32)
+            nc.vector.quantize_mx(out=ow[:].bitcast(FP8X4), scales=o_scales[:, cols[c]], in_=o_bf[c][:].rearrange("p w t -> p (w t)"))
+            nc.sync.dma_start(out_words[:, cols[c]], ow[:].bitcast(I32))
+
+        for i in range(len(CHUNKS) + 2):
+            if i <= last:
+                product(i)
+            if 1 <= i <= last + 1:
+                add_res(i - 1)
+            if i >= 2:
+                planes(i - 2)
+        for q in range(4):
+            queue = nc.sync if q % 2 else nc.scalar
+            queue.dma_start(out_2[0, 4 * q : 4 * q + 4, :].bitcast(I32), o_scales[32 * q : 32 * q + 4, :].bitcast(I32))

@@ -45,6 +45,9 @@ def tile_picked_readkindgpaget_none_po_kernel(
             for q, queue in enumerate(queues):
                 queue.dma_start(tile[32 * q : 32 * q + 4, :].bitcast(I32), src[0, 4 * q : 4 * q + 4, :].bitcast(I32))
 
+        def weave(engine_copy, out, src):
+            engine_copy(out.rearrange("p (c i) t -> p c t i", i=4), src.rearrange("p t (c i) -> p c t i", i=4))
+
         def dealt_rows(src):
             return src.rearrange("(p t) w -> p t w", t=R)
 
@@ -58,7 +61,6 @@ def tile_picked_readkindgpaget_none_po_kernel(
         w2w_raw = sb("w2w_raw", [P, 2 * N], U8)
         xw = sb("xw", [P, T], U32)
         nc.sync.dma_start(w1w_raw[:].bitcast(I32), w1_words[0].bitcast(I32))
-        nc.sync.dma_start(w2w_raw[:].bitcast(I32), w2_words[0].bitcast(I32))
         nc.sync.dma_start(xw[:].bitcast(I32), x_words[0].rearrange("p n t -> p (n t)").bitcast(I32))
         offs_sb = load_list("offs_sb", offs)
         load_scale_rows([nc.sync] * 4, xs, x_scales)
@@ -77,6 +79,7 @@ def tile_picked_readkindgpaget_none_po_kernel(
         page = [sb("page%d" % t, [P, U], F32) for t in range(R)]
         for t in range(R):
             nc.sync.dma_start(page[t][:], dealt_rows(mem)[:, t, :])
+        nc.sync.dma_start(w2w_raw[:].bitcast(I32), w2_words[0].bitcast(I32))
         load_scale_rows([nc.sync] * 4, w2s_raw, w2_scales)
         nc.sync.dma_start(gt_sb[:], gt.rearrange("(p t) o -> p (t o)", t=R))
         starts = [sum(CHUNKS[:c]) for c in range(len(CHUNKS))]
@@ -85,20 +88,19 @@ def tile_picked_readkindgpaget_none_po_kernel(
         for c in range(len(CHUNKS)):
             nc.sync.dma_start(res_sb[c][:], dealt_rows(res)[:, :, cols[c]])
 
-        def deal_fp4_words(name, raw):
-            dealt = sb(name, [P, 2 * R * P], U8)
+        def deal_fp4_words(name, raw, tag=""):
+            dealt = sb(name, [P, 2 * R * P], U8, tag)
             nc.vector.tensor_copy(
-                dealt[:].rearrange("p (t m b) -> p m t b", t=R, b=2), raw[:].rearrange("p (m t b) -> p m t b", t=R, b=2)
+                dealt[:].rearrange("p (t m b) -> p t m b", t=R, b=2), raw[:].rearrange("p (m t b) -> p t m b", t=R, b=2)
             )
             return dealt
 
         def deal_bytes(name, raw, tag=""):
             dealt = sb(name, [P, R * P], U8, tag)
-            nc.vector.tensor_copy(dealt[:].rearrange("p (t m) -> p m t", t=R), raw[:].rearrange("p (m t) -> p m t", t=R))
+            nc.vector.tensor_copy(dealt[:].rearrange("p (t m) -> p t m", t=R), raw[:].rearrange("p (m t) -> p t m", t=R))
             return dealt
 
         w1w = deal_fp4_words("w1w", w1w_raw)
-        w2w = deal_fp4_words("w2w", w2w_raw)
 
         xq_w = sb("xq_w", [P, S], U32)
         xq_s = sb("xq_s", [P, S], U8)
@@ -132,7 +134,7 @@ def tile_picked_readkindgpaget_none_po_kernel(
         nc.vector.tensor_copy(xc_s_raw[:], xs[:].indirect(cand_sb[:]))
         xc_s = deal_bytes("xc_s", xc_s_raw)
 
-        z = [sb("z%d" % h, [P, R, HALF], F32) for h in range(2)]
+        z = [sb("z0", [P, R, HALF], F32)]
         z_bf = [sb("z_bf%d" % h, [P, HALF, R], BF16) for h in range(2)]
         zw = sb("zw", [P, S], U32)
         zs = sb("zs", [P, S], U8)
@@ -153,27 +155,32 @@ def tile_picked_readkindgpaget_none_po_kernel(
             nc.vector.tensor_tensor(z[h][:, t, :], y[t][:].indirect(entries(n2_sb, halves[h])), zt[h, t][:], ALU.add)
 
         def z_round(h):
-            nc.scalar.copy(z_bf[h][:], z[h][:].rearrange("p t j -> p j t"))
+            weave(nc.scalar.copy, z_bf[h][:], z[h][:])
 
         def z_quantize(h):
             nc.vector.quantize_mx(out=zw[:, halves[h]].bitcast(FP8X4), scales=zs[:, halves[h]], in_=z_bf[h][:].rearrange("p j t -> p (j t)"))
 
-        def scores(t, part, b):
+        def scores(tiles, part, banks):
             n = part.stop - part.start
-            acc = bank(b, "s_acc%d_%d" % (t, part.start), [P, n])
-            nc.tensor.matmul_mx(
-                out=acc[:],
-                lhsT=xc_w[:, P * t : P * (t + 1)].bitcast(FP8X4),
-                lhsT_scale=xc_s[:, P * t : P * (t + 1)],
-                rhs=zw[:, part].bitcast(FP8X4),
-                rhs_scale=zs[:, part],
-                start=True,
-                stop=True,
-            )
-            th = sb("th%d_%d" % (t, part.start), [P, n], F32)
-            nc.scalar.activation(fresh[t][:, part], acc[:], ACT.Silu, scale=0.0625)
-            nc.scalar.activation(th[:], acc[:], ACT.Tanh, scale=0.03125)
-            nc.scalar.activation(keepw[t][:, part], th[:], ACT.Copy, scale=-0.5, bias=0.5)
+            acc, th = {}, {}
+            for t, b in zip(tiles, banks):
+                acc[t] = bank(b, "s_acc%d_%d" % (t, part.start), [P, n])
+                th[t] = sb("th%d_%d" % (t, part.start), [P, n], F32)
+                nc.tensor.matmul_mx(
+                    out=acc[t][:],
+                    lhsT=xc_w[:, P * t : P * (t + 1)].bitcast(FP8X4),
+                    lhsT_scale=xc_s[:, P * t : P * (t + 1)],
+                    rhs=zw[:, part].bitcast(FP8X4),
+                    rhs_scale=zs[:, part],
+                    start=True,
+                    stop=True,
+                )
+            nc.scalar.activation(fresh[tiles[0]][:, part], acc[tiles[0]][:], ACT.Silu, scale=0.0625)
+            for t in tiles:
+                nc.scalar.activation(th[t][:], acc[t][:], ACT.Tanh, scale=0.03125)
+            for t in tiles:
+                nc.scalar.activation(keepw[t][:, part], th[t][:], ACT.Copy, scale=-0.5, bias=0.5)
+            nc.scalar.activation(fresh[tiles[1]][:, part], acc[tiles[1]][:], ACT.Silu, scale=0.0625)
 
         for t in range(R + 1):
             if t < R:
@@ -181,18 +188,20 @@ def tile_picked_readkindgpaget_none_po_kernel(
             if t > 0:
                 z_second(0, t - 1)
         z_round(0)
-        for t in range(R - 1):
+        for t in range(R):
             z_first(1, t)
         z_quantize(0)
-        scores(0, first, 4)
-        scores(1, first, 5)
-        z_first(1, R - 1, tag="z_bf0")
+        scores((0, 1), first, (4, 5))
+        z.append(sb("z1", [P, R, HALF], F32, "z_bf0"))
         for t in range(R):
             z_second(1, t)
         z_round(1)
 
         kept = {}
         z2_bf = [sb("z2_bf%d" % c, [P, n, R], BF16) for c, n in enumerate(CHUNKS)]
+        groups = ((0, 1), (2, 3, 4))
+        spans = [slice(cols[g[0]].start, cols[g[-1]].stop) for g in groups]
+        z2_low = [sb("z2_low%d" % g, [P, 2, span.stop - span.start], BF16) for g, span in enumerate(spans)]
 
         def fetch(t, part, tag=""):
             kept[t, part.start] = sb("kept%d_%d" % (t, part.start), [P, part.stop - part.start], F32, tag)
@@ -201,27 +210,36 @@ def tile_picked_readkindgpaget_none_po_kernel(
         def put(t, part):
             nc.vector.tensor_tensor(page[t][:].indirect(entries(n3_sb, part)), kept[t, part.start][:], fresh[t][:, part], ALU.add)
 
-        def z2_round(c, t):
-            nc.scalar.activation(z2_bf[c][:, :, t], page[t][:, cols[c]], ACT.Copy, scale=gt_sb[:, t : t + 1])
+        def z2_round(out, t, slots):
+            nc.scalar.activation(out, page[t][:, slots], ACT.Copy, scale=gt_sb[:, t : t + 1])
 
         fetch(0, first)
         put(0, first)
         z_quantize(1)
-        scores(0, second, 6)
-        scores(1, second, 7)
-        scores(2, whole, 0)
-        scores(3, whole, 1)
+        scores((0, 1), second, (6, 7))
+        scores((2, 3), whole, (0, 1))
         fetch(1, first, tag="z_bf1")
         put(1, first)
-        for pair, part in (((0, 1), second), ((2, 3), whole)):
-            for t in pair:
-                fetch(t, part)
-            for t in pair:
-                put(t, part)
-                if t < R - 1:
-                    for c in range(len(CHUNKS)):
-                        z2_round(c, t)
-        w2s = deal_bytes("w2s", w2s_raw, tag="kept3_0")
+        fetch(0, second)
+        fetch(1, second)
+        put(0, second)
+        for g, span in enumerate(spans):
+            z2_round(z2_low[g][:, 0, :], 0, span)
+        put(1, second)
+        for g, span in enumerate(spans):
+            z2_round(z2_low[g][:, 1, :], 1, span)
+        for g, span in enumerate(spans):
+            for c in groups[g]:
+                low = z2_low[g][:, :, cols[c].start - span.start : cols[c].stop - span.start]
+                nc.scalar.copy(z2_bf[c][:, :, 0:2], low.rearrange("p t w -> p w t"))
+        fetch(2, whole)
+        fetch(3, whole)
+        put(2, whole)
+        for c in range(len(CHUNKS)):
+            z2_round(z2_bf[c][:, :, 2], 2, cols[c])
+        put(3, whole)
+        w2w = deal_fp4_words("w2w", w2w_raw, tag="kept3_0")
+        w2s = deal_bytes("w2s", w2s_raw, tag="fresh3")
 
         out_rows = dealt_rows(out_0)
         out_words = out_1[0].rearrange("p n t -> p (n t)").bitcast(I32)
@@ -234,7 +252,7 @@ def tile_picked_readkindgpaget_none_po_kernel(
         def product(c):
             n = CHUNKS[c]
             per_bank = 512 // n
-            z2_round(c, R - 1)
+            z2_round(z2_bf[c][:, :, R - 1], R - 1, cols[c])
             z2w = sb("z2w%d" % c, [P, n], U32)
             z2s = sb("z2s%d" % c, [P, n], U8)
             nc.vector.quantize_mx(out=z2w[:].bitcast(FP8X4), scales=z2s[:], in_=z2_bf[c][:].rearrange("p j t -> p (j t)"))
@@ -258,10 +276,7 @@ def tile_picked_readkindgpaget_none_po_kernel(
                 rows = slice(t, t + per_bank)
                 nc.vector.tensor_tensor(o32[c][:, rows, :], accs[c, t][:], res_sb[c][:, rows, :], ALU.add)
             nc.sync.dma_start(out_rows[:, :, cols[c]], o32[c][:])
-            if c < last:
-                nc.scalar.copy(o_bf[c][:], o32[c][:].rearrange("p t w -> p w t"))
-            else:
-                nc.vector.tensor_copy(o_bf[c][:], o32[c][:].rearrange("p t w -> p w t"))
+            weave(nc.scalar.copy if c < last else nc.vector.tensor_copy, o_bf[c][:], o32[c][:])
 
         def planes(c):
             ow = sb("ow%d" % c, [P, CHUNKS[c]], U32)

@@ -72,9 +72,9 @@ def tile_picked_readkindgpaget_none_po_kernel(
         n1_sb = load_list("n1_sb", n1)
         n2_sb = load_list("n2_sb", n2)
 
-        tab_raw = [sb("tab_raw%d" % t, [P, J], F32) for t in range(R)]
+        tab_sb = [sb("tab%d" % t, [P, J], F32) for t in range(R)]
         for t in range(R):
-            nc.sync.dma_start(tab_raw[t][:], dealt_rows(tab)[:, t, :])
+            nc.sync.dma_start(tab_sb[t][:], dealt_rows(tab)[:, t, :])
         n3_sb = load_list("n3_sb", n3)
         page = [sb("page%d" % t, [P, U], F32) for t in range(R)]
         for t in range(R):
@@ -110,15 +110,15 @@ def tile_picked_readkindgpaget_none_po_kernel(
 
         gs_half = sb("gs_half", [P, R], F32)
         nc.scalar.mul(gs_half[:], gs_sb[:], -0.5)
-        tab2 = [sb("tab2_%d" % t, [P, J], F32) for t in range(R)]
-        for t in range(R):
-            nc.scalar.mul(tab2[t][:], tab_raw[t][:], -2.0)
 
+        first, second, whole = slice(0, HALF), slice(HALF, S), slice(0, S)
+        halves = (first, second)
         y = [sb("y%d" % t, [P, S], F32) for t in range(R)]
+        own = [[sb("own%d_%d" % (h, t), [P, HALF], F32) for t in range(R)] for h in range(2)]
+        y_acc = [bank(t, "y_acc%d" % t, [P, S]) for t in range(R)]
         for t in range(R):
-            acc = bank(t, "y_acc%d" % t, [P, S])
             nc.tensor.matmul_mx(
-                out=acc[:],
+                out=y_acc[t][:],
                 lhsT=w1w[:, 2 * P * t : 2 * P * (t + 1)].bitcast(FP4X4),
                 lhsT_scale=w1s[:, P * t : P * (t + 1)],
                 rhs=xq_w[:].bitcast(FP8X4),
@@ -126,7 +126,11 @@ def tile_picked_readkindgpaget_none_po_kernel(
                 start=True,
                 stop=True,
             )
-            nc.scalar.activation(y[t][:], acc[:], ACT.Copy, scale=gs_half[:, t : t + 1])
+            nc.scalar.activation(own[0][t][:], y_acc[t][:, first], ACT.Copy, scale=gs_sb[:, t : t + 1])
+        for t in range(R):
+            nc.scalar.activation(y[t][:], y_acc[t][:], ACT.Copy, scale=gs_half[:, t : t + 1])
+        for t in range(R):
+            nc.scalar.activation(own[1][t][:], y_acc[t][:, second], ACT.Copy, scale=gs_sb[:, t : t + 1])
 
         xc_w = sb("xc_w", [P, C], U32)
         xc_s_raw = sb("xc_s_raw", [P, C], U8)
@@ -141,15 +145,13 @@ def tile_picked_readkindgpaget_none_po_kernel(
         zt = {}
         keepw = [sb("keepw%d" % t, [P, S], F32) for t in range(R)]
         fresh = [sb("fresh%d" % t, [P, S], F32) for t in range(R)]
-        first, second, whole = slice(0, HALF), slice(HALF, S), slice(0, S)
-        halves = (first, second)
 
         def entries(lst, part):
             return lst[:, part.start // 16 : part.stop // 16]
 
         def z_first(h, t, tag=""):
             zt[h, t] = sb("zt%d_%d" % (h, t), [P, HALF], F32, tag)
-            nc.vector.tensor_tensor(zt[h, t][:], tab2[t][:].indirect(entries(n1_sb, halves[h])), y[t][:, halves[h]], ALU.mult)
+            nc.vector.tensor_tensor(zt[h, t][:], tab_sb[t][:].indirect(entries(n1_sb, halves[h])), own[h][t][:], ALU.mult)
 
         def z_second(h, t):
             nc.vector.tensor_tensor(z[h][:, t, :], y[t][:].indirect(entries(n2_sb, halves[h])), zt[h, t][:], ALU.add)

@@ -246,6 +246,7 @@ def tile_picked_readkindgpaget_none_po_kernel(
         out_rows = dealt_rows(out_0)
         out_words = out_1[0].rearrange("p n t -> p (n t)").bitcast(I32)
         o_scales = sb("o_scales", [P, U], U8)
+        o_words = sb("o_words", [P, U], U32)
         o32 = [sb("o32_%d" % c, [P, R, n], F32) for c, n in enumerate(CHUNKS)]
         o_bf = [sb("o_bf%d" % c, [P, n, R], BF16) for c, n in enumerate(CHUNKS)]
         accs = {}
@@ -276,14 +277,23 @@ def tile_picked_readkindgpaget_none_po_kernel(
             per_bank = 512 // CHUNKS[c]
             for t in range(0, R, per_bank):
                 rows = slice(t, t + per_bank)
+                if c == last:
+                    nc.vector.tensor_tensor(
+                        o_bf[c][:].rearrange("p (c i) t -> p c t i", i=4),
+                        accs[c, t][:].rearrange("p t (c i) -> p c t i", i=4),
+                        res_sb[c][:].rearrange("p t (c i) -> p c t i", i=4),
+                        ALU.add,
+                    )
                 nc.vector.tensor_tensor(o32[c][:, rows, :], accs[c, t][:], res_sb[c][:, rows, :], ALU.add)
             nc.sync.dma_start(out_rows[:, :, cols[c]], o32[c][:])
-            weave(nc.scalar.copy if c < last else nc.vector.tensor_copy, o_bf[c][:], o32[c][:])
+            if c < last:
+                weave(nc.scalar.copy, o_bf[c][:], o32[c][:])
 
         def planes(c):
-            ow = sb("ow%d" % c, [P, CHUNKS[c]], U32)
-            nc.vector.quantize_mx(out=ow[:].bitcast(FP8X4), scales=o_scales[:, cols[c]], in_=o_bf[c][:].rearrange("p w t -> p (w t)"))
-            nc.sync.dma_start(out_words[:, cols[c]], ow[:].bitcast(I32))
+            nc.vector.quantize_mx(out=o_words[:, cols[c]].bitcast(FP8X4), scales=o_scales[:, cols[c]], in_=o_bf[c][:].rearrange("p w t -> p (w t)"))
+            if c % 2 == 1 or c == last:
+                slots = slice(cols[c - c % 2].start, cols[c].stop)
+                nc.sync.dma_start(out_words[:, slots], o_words[:, slots].bitcast(I32))
 
         for i in range(len(CHUNKS) + 2):
             if i <= last:

from contextlib import ExitStack

import concourse.mybir as mybir

K, T, S, N, H, J, C, U = 512, 2048, 512, 512, 512, 512, 512, 1024
FLOPS = 2 * (K * H * S + K * C * S + C * N * U)

F32 = mybir.dt.float32
BF16 = mybir.dt.bfloat16
I32 = mybir.dt.int32
U32 = mybir.dt.uint32
U16 = mybir.dt.uint16
U8 = mybir.dt.uint8
FP8X4 = mybir.dt.float8_e4m3fn_x4
FP4X4 = mybir.dt.float4_e2m1fn_x4
ALU = mybir.AluOpType
ACT = mybir.ActivationFunctionType

P = 128
R = 4
HALF = S // 2
CHUNKS = (128, 256, 256, 256, 128)


def tile_picked_readkindgpaget_none_po_kernel(
    tc, x_words, x_scales, w1_words, w1_scales, tab, gs, mem, res, gt, w2_words, w2_scales, offs, n1, n2, cand, n3, out_0, out_1, out_2
):
    nc = tc.nc
    with ExitStack() as ctx:
        keep = ctx.enter_context(tc.tile_pool(name="keep", bufs=1))
        psum = ctx.enter_context(tc.psum_pool(name="psum", bufs=1))

        def sb(name, shape, dtype, tag=""):
            return keep.tile(shape, dtype, name=name, tag=tag or name, align_bytes=64)

        def bank(b, name, shape):
            return psum.tile(shape, F32, name=name, tag="bank%d" % b)

        def load_list(name, src):
            tile = sb(name, [P, S // 16], U16)
            nc.sync.dma_start(tile[:], src)
            return tile

        def load_scale_rows(queues, tile, src):
            for q, queue in enumerate(queues):
                queue.dma_start(tile[32 * q : 32 * q + 4, :].bitcast(I32), src[0, 4 * q : 4 * q + 4, :].bitcast(I32))

        def weave(engine_copy, out, src):
            engine_copy(out.rearrange("p (c i) t -> p c t i", i=4), src.rearrange("p t (c i) -> p c t i", i=4))

        def dealt_rows(src):
            return src.rearrange("(p t) w -> p t w", t=R)

        xs = sb("xs", [P, T], U8)
        w1s_raw = sb("w1s_raw", [P, H], U8)
        w2s_raw = sb("w2s_raw", [P, N], U8)
        for tile in (xs, w1s_raw, w2s_raw):
            nc.vector.memset(tile[:].bitcast(I32), 0)

        w1w_raw = sb("w1w_raw", [P, 2 * H], U8)
        w2w_raw = sb("w2w_raw", [P, 2 * N], U8)
        xw = sb("xw", [P, T], U32)
        nc.sync.dma_start(w1w_raw[:].bitcast(I32), w1_words[0].bitcast(I32))
        nc.sync.dma_start(xw[:].bitcast(I32), x_words[0].rearrange("p n t -> p (n t)").bitcast(I32))
        offs_sb = load_list("offs_sb", offs)
        load_scale_rows([nc.sync] * 4, xs, x_scales)
        load_scale_rows([nc.sync, nc.sync, nc.gpsimd, nc.gpsimd], w1s_raw, w1_scales)
        cand_sb = load_list("cand_sb", cand)
        gs_sb = sb("gs_sb", [P, R], F32)
        gt_sb = sb("gt_sb", [P, R], F32)
        nc.sync.dma_start(gs_sb[:], gs.rearrange("(p t) o -> p (t o)", t=R))
        n1_sb = load_list("n1_sb", n1)
        n2_sb = load_list("n2_sb", n2)

        tab_sb = [sb("tab%d" % t, [P, J], F32) for t in range(R)]
        for t in range(R):
            nc.sync.dma_start(tab_sb[t][:], dealt_rows(tab)[:, t, :])
        n3_sb = load_list("n3_sb", n3)
        page = [sb("page%d" % t, [P, U], F32) for t in range(R)]
        for t in range(R):
            nc.sync.dma_start(page[t][:], dealt_rows(mem)[:, t, :])
        nc.sync.dma_start(w2w_raw[:].bitcast(I32), w2_words[0].bitcast(I32))
        load_scale_rows([nc.sync] * 4, w2s_raw, w2_scales)
        nc.sync.dma_start(gt_sb[:], gt.rearrange("(p t) o -> p (t o)", t=R))
        starts = [sum(CHUNKS[:c]) for c in range(len(CHUNKS))]
        cols = [slice(a, a + n) for a, n in zip(starts, CHUNKS)]
        res_sb = [sb("res%d" % c, [P, R, n], F32) for c, n in enumerate(CHUNKS)]
        for c in range(len(CHUNKS)):
            nc.sync.dma_start(res_sb[c][:], dealt_rows(res)[:, :, cols[c]])

        def deal_fp4_words(name, raw, tag=""):
            dealt = sb(name, [P, 2 * R * P], U8, tag)
            nc.vector.tensor_copy(
                dealt[:].rearrange("p (t m b) -> p t m b", t=R, b=2), raw[:].rearrange("p (m t b) -> p t m b", t=R, b=2)
            )
            return dealt

        def deal_bytes(name, raw, tag=""):
            dealt = sb(name, [P, R * P], U8, tag)
            nc.vector.tensor_copy(dealt[:].rearrange("p (t m) -> p t m", t=R), raw[:].rearrange("p (m t) -> p t m", t=R))
            return dealt

        w1w = deal_fp4_words("w1w", w1w_raw)

        xq_w = sb("xq_w", [P, S], U32)
        xq_s = sb("xq_s", [P, S], U8)
        nc.vector.tensor_copy(xq_w[:], xw[:].indirect(offs_sb[:]))
        nc.vector.tensor_copy(xq_s[:], xs[:].indirect(offs_sb[:]))
        w1s = deal_bytes("w1s", w1s_raw)

        gs_half = sb("gs_half", [P, R], F32)
        nc.scalar.mul(gs_half[:], gs_sb[:], -0.5)

        first, second, whole = slice(0, HALF), slice(HALF, S), slice(0, S)
        halves = (first, second)
        y = [sb("y%d" % t, [P, S], F32) for t in range(R)]
        own = [[sb("own%d_%d" % (h, t), [P, HALF], F32) for t in range(R)] for h in range(2)]
        y_acc = [bank(t, "y_acc%d" % t, [P, S]) for t in range(R)]
        for t in range(R):
            nc.tensor.matmul_mx(
                out=y_acc[t][:],
                lhsT=w1w[:, 2 * P * t : 2 * P * (t + 1)].bitcast(FP4X4),
                lhsT_scale=w1s[:, P * t : P * (t + 1)],
                rhs=xq_w[:].bitcast(FP8X4),
                rhs_scale=xq_s[:],
                start=True,
                stop=True,
            )
            nc.scalar.activation(own[0][t][:], y_acc[t][:, first], ACT.Copy, scale=gs_sb[:, t : t + 1])
        for t in range(R):
            nc.scalar.activation(y[t][:], y_acc[t][:], ACT.Copy, scale=gs_half[:, t : t + 1])
        for t in range(R):
            nc.scalar.activation(own[1][t][:], y_acc[t][:, second], ACT.Copy, scale=gs_sb[:, t : t + 1])

        xc_w = sb("xc_w", [P, C], U32)
        xc_s_raw = sb("xc_s_raw", [P, C], U8)
        nc.vector.tensor_copy(xc_w[:].rearrange("p (t m) -> p m t", t=R), xw[:].indirect(cand_sb[:]))
        nc.vector.tensor_copy(xc_s_raw[:], xs[:].indirect(cand_sb[:]))
        xc_s = deal_bytes("xc_s", xc_s_raw)

        z = [sb("z0", [P, R, HALF], F32)]
        z_bf = [sb("z_bf%d" % h, [P, HALF, R], BF16) for h in range(2)]
        zw = sb("zw", [P, S], U32)
        zs = sb("zs", [P, S], U8)
        zt = {}
        keepw = [sb("keepw%d" % t, [P, S], F32) for t in range(R)]
        fresh = [sb("fresh%d" % t, [P, S], F32) for t in range(R)]

        def entries(lst, part):
            return lst[:, part.start // 16 : part.stop // 16]

        def z_first(h, t, tag=""):
            zt[h, t] = sb("zt%d_%d" % (h, t), [P, HALF], F32, tag)
            nc.vector.tensor_tensor(zt[h, t][:], tab_sb[t][:].indirect(entries(n1_sb, halves[h])), own[h][t][:], ALU.mult)

        def z_second(h, t):
            nc.vector.tensor_tensor(z[h][:, t, :], y[t][:].indirect(entries(n2_sb, halves[h])), zt[h, t][:], ALU.add)

        def z_round(h):
            weave(nc.scalar.copy, z_bf[h][:], z[h][:])

        def z_quantize(h):
            nc.vector.quantize_mx(out=zw[:, halves[h]].bitcast(FP8X4), scales=zs[:, halves[h]], in_=z_bf[h][:].rearrange("p j t -> p (j t)"))

        def scores(tiles, part, banks):
            n = part.stop - part.start
            acc, th = {}, {}
            for t, b in zip(tiles, banks):
                acc[t] = bank(b, "s_acc%d_%d" % (t, part.start), [P, n])
                th[t] = sb("th%d_%d" % (t, part.start), [P, n], F32)
                nc.tensor.matmul_mx(
                    out=acc[t][:],
                    lhsT=xc_w[:, P * t : P * (t + 1)].bitcast(FP8X4),
                    lhsT_scale=xc_s[:, P * t : P * (t + 1)],
                    rhs=zw[:, part].bitcast(FP8X4),
                    rhs_scale=zs[:, part],
                    start=True,
                    stop=True,
                )
            nc.scalar.activation(fresh[tiles[0]][:, part], acc[tiles[0]][:], ACT.Silu, scale=0.0625)
            for t in tiles:
                nc.scalar.activation(th[t][:], acc[t][:], ACT.Tanh, scale=0.03125)
            for t in tiles:
                nc.scalar.activation(keepw[t][:, part], th[t][:], ACT.Copy, scale=-0.5, bias=0.5)
            nc.scalar.activation(fresh[tiles[1]][:, part], acc[tiles[1]][:], ACT.Silu, scale=0.0625)

        for t in range(R + 1):
            if t < R:
                z_first(0, t)
            if t > 0:
                z_second(0, t - 1)
        z_round(0)
        for t in range(R):
            z_first(1, t)
        z_quantize(0)
        scores((0, 1), first, (4, 5))
        z.append(sb("z1", [P, R, HALF], F32, "z_bf0"))
        for t in range(R):
            z_second(1, t)
        z_round(1)

        kept = {}
        z2_bf = [sb("z2_bf%d" % c, [P, n, R], BF16) for c, n in enumerate(CHUNKS)]
        groups = ((0, 1), (2, 3, 4))
        spans = [slice(cols[g[0]].start, cols[g[-1]].stop) for g in groups]
        z2_low = [sb("z2_low%d" % g, [P, 2, span.stop - span.start], BF16) for g, span in enumerate(spans)]

        def fetch(t, part, tag=""):
            kept[t, part.start] = sb("kept%d_%d" % (t, part.start), [P, part.stop - part.start], F32, tag)
            nc.vector.tensor_tensor(kept[t, part.start][:], page[t][:].indirect(entries(n3_sb, part)), keepw[t][:, part], ALU.mult)

        def put(t, part):
            nc.vector.tensor_tensor(page[t][:].indirect(entries(n3_sb, part)), kept[t, part.start][:], fresh[t][:, part], ALU.add)

        def z2_round(out, t, slots):
            nc.scalar.activation(out, page[t][:, slots], ACT.Copy, scale=gt_sb[:, t : t + 1])

        fetch(0, first)
        put(0, first)
        z_quantize(1)
        scores((0, 1), second, (6, 7))
        scores((2, 3), whole, (0, 1))
        fetch(1, first, tag="z_bf1")
        put(1, first)
        fetch(0, second)
        fetch(1, second)
        put(0, second)
        for g, span in enumerate(spans):
            z2_round(z2_low[g][:, 0, :], 0, span)
        put(1, second)
        for g, span in enumerate(spans):
            z2_round(z2_low[g][:, 1, :], 1, span)
        for g, span in enumerate(spans):
            for c in groups[g]:
                low = z2_low[g][:, :, cols[c].start - span.start : cols[c].stop - span.start]
                nc.scalar.copy(z2_bf[c][:, :, 0:2], low.rearrange("p t w -> p w t"))
        fetch(2, whole)
        fetch(3, whole)
        put(2, whole)
        for c in range(len(CHUNKS)):
            z2_round(z2_bf[c][:, :, 2], 2, cols[c])
        put(3, whole)
        w2w = deal_fp4_words("w2w", w2w_raw, tag="kept3_0")
        w2s = deal_bytes("w2s", w2s_raw, tag="fresh3")

        out_rows = dealt_rows(out_0)
        out_words = out_1[0].rearrange("p n t -> p (n t)").bitcast(I32)
        o_scales = sb("o_scales", [P, U], U8)
        o_words = sb("o_words", [P, U], U32)
        o32 = [sb("o32_%d" % c, [P, R, n], F32) for c, n in enumerate(CHUNKS)]
        o_bf = [sb("o_bf%d" % c, [P, n, R], BF16) for c, n in enumerate(CHUNKS)]
        accs = {}
        last = len(CHUNKS) - 1

        def product(c):
            n = CHUNKS[c]
            per_bank = 512 // n
            z2_round(z2_bf[c][:, :, R - 1], R - 1, cols[c])
            z2w = sb("z2w%d" % c, [P, n], U32)
            z2s = sb("z2s%d" % c, [P, n], U8)
            nc.vector.quantize_mx(out=z2w[:].bitcast(FP8X4), scales=z2s[:], in_=z2_bf[c][:].rearrange("p j t -> p (j t)"))
            for t in range(R):
                if t % per_bank == 0:
                    acc = bank((2 + len(accs)) % 8, "o_acc%d_%d" % (c, t), [P, per_bank, n])
                    accs[c, t] = acc
                nc.tensor.matmul_mx(
                    out=acc[:, t % per_bank, :],
                    lhsT=w2w[:, 2 * P * t : 2 * P * (t + 1)].bitcast(FP4X4),
                    lhsT_scale=w2s[:, P * t : P * (t + 1)],
                    rhs=z2w[:].bitcast(FP8X4),
                    rhs_scale=z2s[:],
                    start=True,
                    stop=True,
                )

        def add_res(c):
            per_bank = 512 // CHUNKS[c]
            for t in range(0, R, per_bank):
                rows = slice(t, t + per_bank)
                if c == last:
                    nc.vector.tensor_tensor(
                        o_bf[c][:].rearrange("p (c i) t -> p c t i", i=4),
                        accs[c, t][:].rearrange("p t (c i) -> p c t i", i=4),
                        res_sb[c][:].rearrange("p t (c i) -> p c t i", i=4),
                        ALU.add,
                    )
                nc.vector.tensor_tensor(o32[c][:, rows, :], accs[c, t][:], res_sb[c][:, rows, :], ALU.add)
            nc.sync.dma_start(out_rows[:, :, cols[c]], o32[c][:])
            if c < last:
                weave(nc.scalar.copy, o_bf[c][:], o32[c][:])

        def planes(c):
            nc.vector.quantize_mx(out=o_words[:, cols[c]].bitcast(FP8X4), scales=o_scales[:, cols[c]], in_=o_bf[c][:].rearrange("p w t -> p (w t)"))
            if c % 2 == 1 or c == last:
                slots = slice(cols[c - c % 2].start, cols[c].stop)
                nc.sync.dma_start(out_words[:, slots], o_words[:, slots].bitcast(I32))

        for i in range(len(CHUNKS) + 2):
            if i <= last:
                product(i)
            if 1 <= i <= last + 1:
                add_res(i - 1)
            if i >= 2:
                planes(i - 2)
        for q in range(4):
            queue = nc.sync if q % 2 else nc.scalar
            queue.dma_start(out_2[0, 4 * q : 4 * q + 4, :].bitcast(I32), o_scales[32 * q : 32 * q + 4, :].bitcast(I32))
